import numpy as np
import ml_dtypes


def mxq(x, axis, fmt="e4m3"):
    dtype, down = {"e4m3": (ml_dtypes.float8_e4m3fn, 7), "e5m2": (ml_dtypes.float8_e5m2, 14)}[fmt]
    v = np.moveaxis(np.asarray(x, np.float32).astype(ml_dtypes.bfloat16).astype(np.float64), axis, -1)
    blocks = v.reshape(v.shape[:-1] + (-1, 32))
    amax = np.abs(blocks).max(-1, keepdims=True)
    byte = np.maximum(np.where(amax > 0, np.frexp(amax)[1] - 1 + 127, 0) - down, 1)
    scale = np.exp2(byte - 127.0)
    codes = (blocks / scale).astype(np.float32).astype(dtype).astype(np.float64)
    return np.moveaxis((codes * scale).reshape(v.shape), -1, axis)


WIDE = False


def mx_kscale(k):
    if not WIDE:
        return np.ones(k)
    levels = np.array([10, -10, 5, -5, 0])
    if k % 512:
        return np.exp2(np.random.permutation(np.resize(levels, k // 32))).repeat(32)
    a = np.empty((k // 512, 16))
    for p in range(k // 512):
        a[p, :8] = np.random.permutation(np.resize(levels, 8))
        for g in range(8):
            far = levels[np.abs(levels - a[p, g]) >= 10]
            a[p, g + 8] = far[np.random.randint(len(far))]
    return np.exp2(a.ravel()).repeat(32)


def f64(x):
    return np.asarray(x).astype(np.float64)


def striped(idx):
    return np.tile(idx.reshape(-1, 16).T, (8, 1)).astype(np.uint16)


def unstriped(offs):
    return offs[:16].T.reshape(-1).astype(np.int64)


def striped8(idx):
    return np.concatenate([x.reshape(-1, 16).T for x in idx]).astype(np.uint16)


def runs(offs, k):
    lists = np.stack([offs[16 * r : 16 * r + 16].T.reshape(-1) for r in range(8)]).astype(np.int64)
    return lists[np.arange(k) % 512 // 64]


def pack_weight(w):
    k, n = w.shape
    w = f64(np.asarray(w, np.float32).astype(ml_dtypes.bfloat16)).reshape(k // 32, 32, n)
    amax = np.abs(w).max(1)
    byte = np.clip(np.where(amax > 0, np.frexp(amax)[1] - 1 + 127 - 7, 1), 1, 254)
    scaled = (w * np.exp2(127.0 - byte)[:, None, :]).reshape(k, n).astype(np.float32)
    words = np.ascontiguousarray(scaled.reshape(k // 512, 128, 4, n).transpose(0, 1, 3, 2)).astype(ml_dtypes.float8_e4m3fn).view(np.uint8)
    return words, np.ascontiguousarray(byte.astype(np.uint8).reshape(k // 512, 16, n))


def unpack_weight(words, scales):
    g, p, n, _ = words.shape
    vals = np.ascontiguousarray(words).view(ml_dtypes.float8_e4m3fn).astype(np.float64) * np.repeat(np.exp2(scales.astype(np.float64) - 127.0), 8, axis=1)[..., None]
    return vals.transpose(0, 1, 3, 2).reshape(g * 512, n)


def relu(v):
    return np.maximum(v, 0.0)


K, T, S, N, H = 512, 2048, 512, 512, 512


def setup_inputs():
    n = np.random.standard_normal
    s = mx_kscale(K)[:, None]
    u = mx_kscale(H)
    packed_xT = pack_weight(n((K, T)) * s)
    return {
        "x_words": packed_xT[0],
        "x_scales": packed_xT[1],
        "w1": (n((K, H)) / np.sqrt(K) / s).astype(np.float32),
        "gn": (np.random.uniform(0.5, 1.5, (H, 1)) * u[:, None]).astype(np.float32),
        "w2": (n((H, N)) / np.sqrt(H) / u[:, None]).astype(np.float32),
        "offs": striped(np.random.permutation(T)[:S]),
        "t1": striped8(np.stack([np.random.permutation(S) for _ in range(8)])),
        "t2": striped8(np.stack([np.random.permutation(S) for _ in range(8)])),
        "t3": striped8(np.stack([np.random.permutation(S) for _ in range(8)])),
        "t4": striped8(np.stack([np.random.permutation(S) for _ in range(8)])),
    }


def reference(x_words, x_scales, w1, gn, w2, offs, t1, t2, t3, t4):
    xq = unpack_weight(x_words, x_scales)[:, unstriped(offs)]
    y = mxq(f64(w1), 0, "e4m3").T @ xq
    d1 = y[np.arange(H)[:, None], runs(t1, H)] - (y[np.arange(H)[:, None], runs(t2, H)])
    d2 = y[np.arange(H)[:, None], runs(t2, H)] - (y[np.arange(H)[:, None], runs(t3, H)])
    d3 = y[np.arange(H)[:, None], runs(t3, H)] - (y[np.arange(H)[:, None], runs(t4, H)])
    up = relu(d1) + relu(d2) + relu(d3)
    z = f64(gn) * (up / (np.abs(d1) + np.abs(d2) + np.abs(d3) + 0.25))
    return mxq(f64(w2), 0, "e4m3").T @ mxq(z, 0, "e4m3")

@@ -1,0 +1,227 @@
+from contextlib import ExitStack
+
+import concourse.mybir as mybir
+from concourse.masks import make_identity
+
+K, T, S, N, H = 512, 2048, 512, 512, 512
+FLOPS = 2 * K * H * S + 2 * H * N * S
+
+F32 = mybir.dt.float32
+BF16 = mybir.dt.bfloat16
+I32 = mybir.dt.int32
+U32 = mybir.dt.uint32
+U16 = mybir.dt.uint16
+U8 = mybir.dt.uint8
+FP8X4 = mybir.dt.float8_e4m3fn_x4
+ALU = mybir.AluOpType
+ACT = mybir.ActivationFunctionType
+
+P = 128
+PACK = 4
+HALF = S // 2
+BLOCK = 256
+CHUNKS = (256, 128, 128)
+W1_SPLIT = 40
+STEPS = (("b", 0, (0,)), ("b", 0, (1,)), ("b", 0, (2,)), ("b", 0, (3,)), ("b", 1, (0, 1,)), ("b", 1, (2, 3,)), ("w",), ("f", 0), ("b", 2, (0, 1,)), ("b", 2, (2, 3,)), ("f", 1), ("f", 2))
+S_MODE = "gps"
+
+
+def tile_picked_rsi4_none_p_kernel(tc, x_words, x_scales, w1, gn, w2, offs, t1, t2, t3, t4, out):
+    nc = tc.nc
+    with ExitStack() as ctx:
+        keep = ctx.enter_context(tc.tile_pool(name="keep", bufs=1))
+        ring = ctx.enter_context(tc.tile_pool(name="ring", bufs=2))
+        work = ctx.enter_context(tc.tile_pool(name="work", bufs=3))
+        psum = ctx.enter_context(tc.psum_pool(name="psum", bufs=1))
+
+        def bank(tag):
+            return psum.tile([P, 512], F32, name=tag, tag=tag, bufs={"pb": 1, "rb": 1, "qu": 4, "acc": 2}[tag])
+
+        offs_sb = keep.tile([P, S // 16], U16, name="offs_sb")
+        nc.sync.dma_start(offs_sb[:], offs)
+        xw = keep.tile([P, T], I32, name="xw", align_bytes=64)
+        nc.sync.dma_start(xw[:], x_words[0].rearrange("p n t -> p (n t)").bitcast(I32))
+        xs = keep.tile([P, T], U8, name="xs", align_bytes=64)
+        nc.vector.memset(xs[:].bitcast(I32), 0)
+        for q in range(4):
+            nc.sync.dma_start(xs[32 * q : 32 * q + 4, :].bitcast(I32), x_scales[0][4 * q : 4 * q + 4, :].bitcast(I32))
+        w1_rows = w1.rearrange("(p j) c -> p j c", j=PACK)
+        w1_raw = []
+        for h in range(2):
+            raw = keep.tile([P, PACK, H // 2], F32, name="w1_raw%d" % h, tag="raw%d" % h)
+            nc.sync.dma_start(raw[:], w1_rows[:, :, h * (H // 2) : (h + 1) * (H // 2)])
+            w1_raw.append(raw)
+        lists = [keep.tile([P, S // 16], U16, name="list%d" % i) for i in range(4)]
+        for i, src in ((1, t2), (2, t3), (0, t1), (3, t4)):
+            nc.sync.dma_start(lists[i][:], src)
+        gain = keep.tile([P, PACK], F32, name="gain")
+        nc.sync.dma_start(gain[:], gn.rearrange("(p t) o -> p (t o)", t=PACK))
+
+        warm = keep.tile([P, 1], F32, name="warm")
+        warm2 = keep.tile([P, 1], F32, name="warm2")
+        nc.vector.memset(warm[:], 1.0)
+        nc.scalar.activation(warm2[:], warm[:], ACT.Abs_reciprocal_sqrt)
+        ident = keep.tile([P, P], F32, name="ident", align_bytes=64)
+        make_identity(nc, ident[:])
+
+        xw_pick = keep.tile([P, S], U32, name="xw_pick", align_bytes=64)
+        nc.vector.tensor_copy(xw_pick[:], xw[:].bitcast(U32).indirect(offs_sb[:]))
+        xs_pick = keep.tile([P, S], U8, name="xs_pick", align_bytes=64)
+        nc.vector.tensor_copy(xs_pick[:], xs[:].indirect(offs_sb[:]))
+
+        w1_bf = keep.tile([P, PACK * H], BF16, name="w1_bf", align_bytes=64)
+        w1_view = w1_bf[:].rearrange("p (t m j) -> p m j t", t=PACK, j=PACK)
+        w1_src = [raw[:].rearrange("p j (m t) -> p m j t", t=PACK) for raw in w1_raw]
+        nc.scalar.copy(w1_view[:, 0:64], w1_src[0])
+        nc.vector.tensor_copy(w1_view[:, 64 : 64 + W1_SPLIT], w1_src[1][:, 0:W1_SPLIT])
+        nc.scalar.copy(w1_view[:, 64 + W1_SPLIT : 128], w1_src[1][:, W1_SPLIT:64])
+        w1_codes = keep.tile([P, H], U32, name="w1_codes", align_bytes=64)
+        w1_scales = keep.tile([P, H], U8, name="w1_scales", align_bytes=64)
+        for f0, f1 in ((0, P), (P, 2 * P), (2 * P, 4 * P)):
+            nc.vector.quantize_mx(out=w1_codes[:, f0:f1].bitcast(FP8X4), scales=w1_scales[:, f0:f1], in_=w1_bf[:, PACK * f0 : PACK * f1])
+
+        w2_raw = keep.tile([P, PACK, N], F32, name="w2_raw", tag="raw0")
+        nc.sync.dma_start(w2_raw[:], w2.rearrange("(p j) c -> p j c", j=PACK))
+
+        y = [keep.tile([P, S], F32, name="y%d" % t) for t in range(PACK)]
+        yn = [keep.tile([P, S], F32, name="yn%d" % t) for t in range(PACK)] if S_MODE == "fused" else None
+        for h in range(2):
+            cols = slice(h * HALF, (h + 1) * HALF)
+            acc = bank("acc")
+            nc.tensor.matmul_mx(
+                out=acc[:, 0:HALF], lhsT=w1_codes[:, 0:P].bitcast(FP8X4), lhsT_scale=w1_scales[:, 0:P],
+                rhs=xw_pick[:, cols].bitcast(FP8X4), rhs_scale=xs_pick[:, cols], start=True, stop=True,
+            )
+            if h == 0:
+                nc.scalar.copy(y[0][:, cols], acc[:, 0:HALF])
+            else:
+                nc.vector.tensor_copy(y[0][:, cols], acc[:, 0:HALF])
+            if S_MODE == "fused":
+                nc.scalar.activation(yn[0][:, cols], acc[:, 0:HALF], ACT.Copy, scale=-1.0)
+        for t in range(1, PACK):
+            acc = bank("qu")
+            feats = slice(t * P, (t + 1) * P)
+            nc.tensor.matmul_mx(
+                out=acc[:], lhsT=w1_codes[:, feats].bitcast(FP8X4), lhsT_scale=w1_scales[:, feats],
+                rhs=xw_pick[:].bitcast(FP8X4), rhs_scale=xs_pick[:], start=True, stop=True,
+            )
+            nc.scalar.copy(y[t][:], acc[:])
+            if S_MODE == "fused":
+                nc.scalar.activation(yn[t][:], acc[:], ACT.Copy, scale=-1.0)
+
+        out_rows = out.rearrange("(mt p) j -> p mt j", p=P)
+
+        def add_transposed(dst, terms, cells):
+            for i, term in enumerate(terms):
+                for c in range(cells):
+                    cell = slice(c * P, (c + 1) * P)
+                    nc.tensor.matmul(
+                        dst[:, cell], lhsT=term[:, cell], rhs=ident[:], is_transpose=True,
+                        start=(i == 0 and c == 0), stop=(i == len(terms) - 1 and c == cells - 1),
+                    )
+
+        def block(j0, width, planes, z_planes):
+            size = width * len(planes)
+            cells = size // P
+            early = ring.tile([P, 4, size], F32, name="early")
+            third = ring.tile([P, size], F32, name="third")
+            last = ring.tile([P, size], F32, name="last")
+            ncc, up_q, up_p, up_r = early[:, 1, :], early[:, 2, :], early[:, 3, :], early[:, 1, :]
+            d = last[:]
+            lc = slice(j0 // 16, (j0 + width) // 16)
+            spans = [slice(i * width, (i + 1) * width) for i in range(len(planes))]
+            if S_MODE == "fused":
+                na, b = early[:, 0, :], third[:]
+                for t, sp in zip(planes, spans):
+                    nc.vector.tensor_scalar(na[:, sp], y[t][:].indirect(lists[0][:, lc]), -1.0, 0.0, ALU.mult, ALU.add)
+                for t, sp in zip(planes, spans):
+                    nc.vector.tensor_tensor(ncc[:, sp], yn[t][:].indirect(lists[2][:, lc]), na[:, sp], ALU.subtract)
+                for t, sp in zip(planes, spans):
+                    nc.vector.tensor_tensor(b[:, sp], y[t][:].indirect(lists[1][:, lc]), na[:, sp], ALU.add)
+                for t, sp in zip(planes, spans):
+                    nc.vector.tensor_tensor(d[:, sp], y[t][:].indirect(lists[3][:, lc]), na[:, sp], ALU.add)
+                s = d
+            else:
+                b, na = early[:, 0, :], third[:]
+                for t, sp in zip(planes, spans):
+                    nc.vector.tensor_copy(b[:, sp], y[t][:].indirect(lists[1][:, lc]))
+                for t, sp in zip(planes, spans):
+                    nc.vector.tensor_scalar(ncc[:, sp], y[t][:].indirect(lists[2][:, lc]), -1.0, 0.0, ALU.mult, ALU.add)
+                for t, sp in zip(planes, spans):
+                    nc.vector.tensor_scalar(na[:, sp], y[t][:].indirect(lists[0][:, lc]), -1.0, 0.0, ALU.mult, ALU.add)
+                for t, sp in zip(planes, spans):
+                    nc.vector.tensor_copy(d[:, sp], y[t][:].indirect(lists[3][:, lc]))
+            qu = bank("qu")
+            pb = bank("pb")
+            rb = bank("rb")
+            add_transposed(qu[:, 0:size], [ncc, b] if S_MODE == "fused" else [b, ncc], cells)
+            nc.scalar.activation(up_q, qu[:, 0:size], ACT.Relu)
+            add_transposed(pb[:, 0:size], [b] if S_MODE == "fused" else [b, na], cells)
+            nc.scalar.activation(up_p, pb[:, 0:size], ACT.Relu, scale=-1.0)
+            add_transposed(rb[:, 0:size], [ncc, d], cells)
+            nc.scalar.activation(up_r, rb[:, 0:size], ACT.Relu, scale=-1.0)
+            if S_MODE != "fused":
+                s = na
+                if S_MODE == "gps":
+                    nc.gpsimd.tensor_tensor(s, d, na, ALU.add)
+                else:
+                    nc.vector.tensor_tensor(s, d, na, ALU.add)
+            up = qu[:, BLOCK : BLOCK + size]
+            add_transposed(up, [up_q, up_p, up_r], cells)
+            den = third
+            nc.vector.scalar_tensor_tensor(den[:], up, 2.0, s, ALU.mult, ALU.add)
+            root = last
+            nc.scalar.activation(root[:], den[:], ACT.Abs_reciprocal_sqrt, bias=0.25)
+            rec = work.tile([P, size], F32, name="rec")
+            nc.scalar.activation(rec[:], root[:], ACT.Square)
+            for t, sp in zip(planes, spans):
+                nc.vector.scalar_tensor_tensor(z_planes[:, t, :], up[:, sp], gain[:, t : t + 1], rec[:, sp], ALU.mult, ALU.mult)
+
+        w2_bf = keep.tile([P, N, PACK], BF16, name="w2_bf", align_bytes=64)
+        w2_codes = keep.tile([P, N], U32, name="w2_codes", align_bytes=64)
+        w2_scales = keep.tile([P, N], U8, name="w2_scales", align_bytes=64)
+
+        def quantise_w2():
+            for mt in range(N // P):
+                cols = slice(mt * P, (mt + 1) * P)
+                nc.scalar.copy(w2_bf[:, cols, :].rearrange("p (c i) j -> p c j i", i=4), w2_raw[:, :, cols].rearrange("p j (c i) -> p c j i", i=4))
+            nc.vector.quantize_mx(out=w2_codes[:].bitcast(FP8X4), scales=w2_scales[:], in_=w2_bf[:].rearrange("p c j -> p (c j)"))
+
+        def finish(ci, j0, width, z_planes):
+            last_chunk = ci == len(CHUNKS) - 1
+            z_bf = keep.tile([P, width, PACK], BF16, name="z_bf%d" % ci, align_bytes=64)
+            dst = z_bf[:].rearrange("p (c i) t -> p c t i", i=4)
+            src = z_planes[:].rearrange("p t (c i) -> p c t i", i=4)
+            if last_chunk:
+                nc.vector.tensor_copy(dst, src)
+            else:
+                nc.scalar.copy(dst, src)
+            z_codes = keep.tile([P, width], U32, name="z_codes%d" % ci, align_bytes=64)
+            z_scales = keep.tile([P, width], U8, name="z_scales%d" % ci, align_bytes=64)
+            nc.vector.quantize_mx(out=z_codes[:].bitcast(FP8X4), scales=z_scales[:], in_=z_bf[:].rearrange("p c t -> p (c t)"))
+            per_bank = 2 if last_chunk else 512 // width
+            for m0 in range(0, N // P, per_bank):
+                acc = bank("acc")
+                res = keep.tile([P, per_bank, width], F32, name="res%d_%d" % (ci, m0))
+                for i in range(per_bank):
+                    rows = slice((m0 + i) * P, (m0 + i + 1) * P)
+                    nc.tensor.matmul_mx(
+                        out=acc[:, i * width : (i + 1) * width], lhsT=w2_codes[:, rows].bitcast(FP8X4), lhsT_scale=w2_scales[:, rows],
+                        rhs=z_codes[:].bitcast(FP8X4), rhs_scale=z_scales[:], start=True, stop=True,
+                    )
+                flat = res[:].rearrange("p m j -> p (m j)")
+                if last_chunk and m0 > 0:
+                    nc.vector.tensor_copy(flat, acc[:, 0 : per_bank * width])
+                else:
+                    nc.scalar.copy(flat, acc[:, 0 : per_bank * width])
+                nc.sync.dma_start(out_rows[:, m0 : m0 + per_bank, j0 : j0 + width], res[:])
+
+        z_all = [keep.tile([P, PACK, width], BF16, name="z_planes%d" % ci) for ci, width in enumerate(CHUNKS)]
+        starts = [sum(CHUNKS[:ci]) for ci in range(len(CHUNKS))]
+        for step in STEPS:
+            if step[0] == "b":
+                block(starts[step[1]], CHUNKS[step[1]], step[2], z_all[step[1]])
+            elif step[0] == "w":
+                quantise_w2()
+            else:
+                finish(step[1], starts[step[1]], CHUNKS[step[1]], z_all[step[1]])

@@ -22,20 +22,19 @@ HALF = S // 2
 BLOCK = 256
 CHUNKS = (256, 128, 128)
 W1_SPLIT = 40
-STEPS = (("b", 0, (0,)), ("b", 0, (1,)), ("b", 0, (2,)), ("b", 0, (3,)), ("b", 1, (0, 1,)), ("b", 1, (2, 3,)), ("w",), ("f", 0), ("b", 2, (0, 1,)), ("b", 2, (2, 3,)), ("f", 1), ("f", 2))
-S_MODE = "gps"
+BLOCKS = ((0, (0,)), (0, (1,)), (0, (2,)), (0, (3,)), (1, (0, 1)), (1, (2, 3)), (2, (0, 1)), (2, (2, 3)))
+LAG = 2
 
 
 def tile_picked_rsi4_none_p_kernel(tc, x_words, x_scales, w1, gn, w2, offs, t1, t2, t3, t4, out):
     nc = tc.nc
     with ExitStack() as ctx:
         keep = ctx.enter_context(tc.tile_pool(name="keep", bufs=1))
-        ring = ctx.enter_context(tc.tile_pool(name="ring", bufs=2))
         work = ctx.enter_context(tc.tile_pool(name="work", bufs=3))
         psum = ctx.enter_context(tc.psum_pool(name="psum", bufs=1))
 
         def bank(tag):
-            return psum.tile([P, 512], F32, name=tag, tag=tag, bufs={"pb": 1, "rb": 1, "qu": 4, "acc": 2}[tag])
+            return psum.tile([P, 512], F32, name=tag, tag=tag, bufs={"pr": 2, "rb": 1, "qu": 3, "acc": 2}[tag])
 
         offs_sb = keep.tile([P, S // 16], U16, name="offs_sb")
         nc.sync.dma_start(offs_sb[:], offs)
@@ -57,6 +56,8 @@ def tile_picked_rsi4_none_p_kernel(tc, x_words, x_scales, w1, gn, w2, offs, t1, 
         gain = keep.tile([P, PACK], F32, name="gain")
         nc.sync.dma_start(gain[:], gn.rearrange("(p t) o -> p (t o)", t=PACK))
 
+        ngain = keep.tile([P, PACK], F32, name="ngain")
+        nc.gpsimd.tensor_scalar(ngain[:], gain[:], -1.0, 0.0, ALU.mult, ALU.add)
         warm = keep.tile([P, 1], F32, name="warm")
         warm2 = keep.tile([P, 1], F32, name="warm2")
         nc.vector.memset(warm[:], 1.0)
@@ -84,7 +85,8 @@ def tile_picked_rsi4_none_p_kernel(tc, x_words, x_scales, w1, gn, w2, offs, t1, 
         nc.sync.dma_start(w2_raw[:], w2.rearrange("(p j) c -> p j c", j=PACK))
 
         y = [keep.tile([P, S], F32, name="y%d" % t) for t in range(PACK)]
-        yn = [keep.tile([P, S], F32, name="yn%d" % t) for t in range(PACK)] if S_MODE == "fused" else None
+        yn = [keep.tile([P, S], F32, name="yn%d" % t) for t in range(PACK)]
+        halves = []
         for h in range(2):
             cols = slice(h * HALF, (h + 1) * HALF)
             acc = bank("acc")
@@ -96,18 +98,22 @@ def tile_picked_rsi4_none_p_kernel(tc, x_words, x_scales, w1, gn, w2, offs, t1, 
                 nc.scalar.copy(y[0][:, cols], acc[:, 0:HALF])
             else:
                 nc.vector.tensor_copy(y[0][:, cols], acc[:, 0:HALF])
-            if S_MODE == "fused":
-                nc.scalar.activation(yn[0][:, cols], acc[:, 0:HALF], ACT.Copy, scale=-1.0)
-        for t in range(1, PACK):
-            acc = bank("qu")
+            halves.append((cols, acc))
+        for cols, acc in halves:
+            nc.scalar.activation(yn[0][:, cols], acc[:, 0:HALF], ACT.Copy, scale=-1.0)
+        def project(t, tag):
+            acc = bank(tag)
             feats = slice(t * P, (t + 1) * P)
             nc.tensor.matmul_mx(
                 out=acc[:], lhsT=w1_codes[:, feats].bitcast(FP8X4), lhsT_scale=w1_scales[:, feats],
                 rhs=xw_pick[:].bitcast(FP8X4), rhs_scale=xs_pick[:], start=True, stop=True,
             )
             nc.scalar.copy(y[t][:], acc[:])
-            if S_MODE == "fused":
-                nc.scalar.activation(yn[t][:], acc[:], ACT.Copy, scale=-1.0)
+            nc.scalar.activation(yn[t][:], acc[:], ACT.Copy, scale=-1.0)
+
+        project(1, "qu")
+
+        project(3, "qu")
 
         out_rows = out.rearrange("(mt p) j -> p mt j", p=P)
 
@@ -120,62 +126,97 @@ def tile_picked_rsi4_none_p_kernel(tc, x_words, x_scales, w1, gn, w2, offs, t1, 
                         start=(i == 0 and c == 0), stop=(i == len(terms) - 1 and c == cells - 1),
                     )
 
-        def block(j0, width, planes, z_planes):
-            size = width * len(planes)
+        def cut(k):
+            ci, planes = BLOCKS[k]
+            width = CHUNKS[ci]
+            lc = slice(starts[ci] // 16, (starts[ci] + width) // 16)
+            return [(t, slice(i * width, (i + 1) * width), lc) for i, t in enumerate(planes)], width * len(planes)
+
+        count = len(BLOCKS)
+        def scratch(name):
+            return [keep.tile([P, BLOCK], F32, name="%s%d" % (name, k)) for k in range(count)]
+        def after(older, lag, name):
+            return [older[k - lag] if k >= lag else keep.tile([P, BLOCK], F32, name="%s%d" % (name, k)) for k in range(count)]
+        up_r, den, root, rec = scratch("up_r"), scratch("den"), scratch("root"), scratch("rec")
+        ba = after(den, 3, "ba")
+        ac = after(root, 3, "ac")
+        da = after(up_r, 2, "da")
+        na = after(ac, 2, "na")
+
+        held = {}
+
+        def gather_a(k):
+            for t, sp, lc in cut(k)[0]:
+                nc.vector.tensor_scalar(na[k][:, sp], y[t][:].indirect(lists[0][:, lc]), -1.0, 0.0, ALU.mult, ALU.add)
+
+        def front(k):
+            spans, size = cut(k)
             cells = size // P
-            early = ring.tile([P, 4, size], F32, name="early")
-            third = ring.tile([P, size], F32, name="third")
-            last = ring.tile([P, size], F32, name="last")
-            ncc, up_q, up_p, up_r = early[:, 1, :], early[:, 2, :], early[:, 3, :], early[:, 1, :]
-            d = last[:]
-            lc = slice(j0 // 16, (j0 + width) // 16)
-            spans = [slice(i * width, (i + 1) * width) for i in range(len(planes))]
-            if S_MODE == "fused":
-                na, b = early[:, 0, :], third[:]
-                for t, sp in zip(planes, spans):
-                    nc.vector.tensor_scalar(na[:, sp], y[t][:].indirect(lists[0][:, lc]), -1.0, 0.0, ALU.mult, ALU.add)
-                for t, sp in zip(planes, spans):
-                    nc.vector.tensor_tensor(ncc[:, sp], yn[t][:].indirect(lists[2][:, lc]), na[:, sp], ALU.subtract)
-                for t, sp in zip(planes, spans):
-                    nc.vector.tensor_tensor(b[:, sp], y[t][:].indirect(lists[1][:, lc]), na[:, sp], ALU.add)
-                for t, sp in zip(planes, spans):
-                    nc.vector.tensor_tensor(d[:, sp], y[t][:].indirect(lists[3][:, lc]), na[:, sp], ALU.add)
-                s = d
-            else:
-                b, na = early[:, 0, :], third[:]
-                for t, sp in zip(planes, spans):
-                    nc.vector.tensor_copy(b[:, sp], y[t][:].indirect(lists[1][:, lc]))
-                for t, sp in zip(planes, spans):
-                    nc.vector.tensor_scalar(ncc[:, sp], y[t][:].indirect(lists[2][:, lc]), -1.0, 0.0, ALU.mult, ALU.add)
-                for t, sp in zip(planes, spans):
-                    nc.vector.tensor_scalar(na[:, sp], y[t][:].indirect(lists[0][:, lc]), -1.0, 0.0, ALU.mult, ALU.add)
-                for t, sp in zip(planes, spans):
-                    nc.vector.tensor_copy(d[:, sp], y[t][:].indirect(lists[3][:, lc]))
+            for t, sp, lc in spans:
+                nc.vector.tensor_tensor(ba[k][:, sp], y[t][:].indirect(lists[1][:, lc]), na[k][:, sp], ALU.add)
+            for t, sp, lc in spans:
+                nc.vector.tensor_tensor(ac[k][:, sp], yn[t][:].indirect(lists[2][:, lc]), na[k][:, sp], ALU.subtract)
+            pr = bank("pr")
             qu = bank("qu")
-            pb = bank("pb")
-            rb = bank("rb")
-            add_transposed(qu[:, 0:size], [ncc, b] if S_MODE == "fused" else [b, ncc], cells)
-            nc.scalar.activation(up_q, qu[:, 0:size], ACT.Relu)
-            add_transposed(pb[:, 0:size], [b] if S_MODE == "fused" else [b, na], cells)
-            nc.scalar.activation(up_p, pb[:, 0:size], ACT.Relu, scale=-1.0)
-            add_transposed(rb[:, 0:size], [ncc, d], cells)
-            nc.scalar.activation(up_r, rb[:, 0:size], ACT.Relu, scale=-1.0)
-            if S_MODE != "fused":
-                s = na
-                if S_MODE == "gps":
-                    nc.gpsimd.tensor_tensor(s, d, na, ALU.add)
-                else:
-                    nc.vector.tensor_tensor(s, d, na, ALU.add)
-            up = qu[:, BLOCK : BLOCK + size]
-            add_transposed(up, [up_q, up_p, up_r], cells)
-            den = third
-            nc.vector.scalar_tensor_tensor(den[:], up, 2.0, s, ALU.mult, ALU.add)
-            root = last
-            nc.scalar.activation(root[:], den[:], ACT.Abs_reciprocal_sqrt, bias=0.25)
-            rec = work.tile([P, size], F32, name="rec")
-            nc.scalar.activation(rec[:], root[:], ACT.Square)
-            for t, sp in zip(planes, spans):
-                nc.vector.scalar_tensor_tensor(z_planes[:, t, :], up[:, sp], gain[:, t : t + 1], rec[:, sp], ALU.mult, ALU.mult)
+            ups = work.tile([P, 2, BLOCK], F32, name="ups")
+            add_transposed(pr[:, 0:size], [ba[k]], cells)
+            nc.scalar.activation(ups[:, 0, 0:size], pr[:, 0:size], ACT.Relu, scale=-1.0)
+            add_transposed(qu[:, 0:size], [ba[k], ac[k]], cells)
+            nc.scalar.activation(ups[:, 1, 0:size], qu[:, 0:size], ACT.Relu)
+            held[k] = (pr, qu, ups)
+
+        def back(k):
+            spans, size = cut(k)
+            cells = size // P
+            pr, qu, ups = held[k]
+            pr = bank("rb")
+            for t, sp, lc in spans:
+                nc.vector.tensor_tensor(da[k][:, sp], y[t][:].indirect(lists[3][:, lc]), na[k][:, sp], ALU.add)
+            add_transposed(pr[:, BLOCK : BLOCK + size], [ac[k], da[k]], cells)
+            nc.scalar.activation(up_r[k][:, 0:size], pr[:, BLOCK : BLOCK + size], ACT.Relu, scale=-1.0)
+            add_transposed(qu[:, BLOCK : BLOCK + size], [ups[:, 0, :], ups[:, 1, :], up_r[k]], cells)
+
+        def invert(k):
+            size = cut(k)[1]
+            up = held[k][1][:, BLOCK : BLOCK + size]
+            nc.vector.scalar_tensor_tensor(den[k][:, 0:size], up, 2.0, da[k][:, 0:size], ALU.mult, ALU.add)
+            nc.scalar.activation(root[k][:, 0:size], den[k][:, 0:size], ACT.Abs_reciprocal_sqrt, bias=0.25)
+            nc.scalar.activation(rec[k][:, 0:size], root[k][:, 0:size], ACT.Square)
+
+        def scale(k):
+            spans, size = cut(k)
+            up = held[k][1][:, BLOCK : BLOCK + size]
+            for t, sp, lc in spans:
+                nc.vector.scalar_tensor_tensor(z_all[BLOCKS[k][0]][:, t, :], up[:, sp], gain[:, t : t + 1], rec[k][:, sp], ALU.mult, ALU.mult)
+
+        def close_early(k):
+            size = cut(k)[1]
+            pr, qu, ups = held[k]
+            add_transposed(qu[:, BLOCK : BLOCK + size], [ups[:, 0, :], ups[:, 1, :]], size // P)
+
+        def short_ratio(k):
+            spans, size = cut(k)
+            part = held[k][1][:, BLOCK : BLOCK + size]
+            dc, down = up_r[k], rec[k]
+            for t, sp, lc in spans:
+                nc.vector.tensor_tensor(da[k][:, sp], y[t][:].indirect(lists[3][:, lc]), na[k][:, sp], ALU.add)
+            for t, sp, lc in spans:
+                nc.vector.tensor_tensor(dc[:, sp], da[k][:, sp], ac[k][:, sp], ALU.add)
+            for t, sp, lc in spans:
+                nc.vector.scalar_tensor_tensor(down[:, sp], dc[:, sp], 0.0, part[:, sp], ALU.min, ALU.subtract)
+            for t, sp, lc in spans:
+                nc.vector.scalar_tensor_tensor(den[k][:, sp], down[:, sp], -2.0, da[k][:, sp], ALU.mult, ALU.add)
+            for t, sp, lc in spans:
+                nc.scalar.activation(root[k][:, sp], den[k][:, sp], ACT.Abs_reciprocal_sqrt, bias=0.25)
+
+        def short_scale(k, z_bf):
+            spans, size = cut(k)
+            down, once = rec[k], up_r[k]
+            for t, sp, lc in spans:
+                nc.vector.scalar_tensor_tensor(once[:, sp], down[:, sp], ngain[:, t : t + 1], root[k][:, sp], ALU.mult, ALU.mult)
+            t0 = spans[0][0]
+            pairs = "p (t j) -> p j t"
+            nc.vector.tensor_tensor(z_bf[:, :, t0 : t0 + 2], once[:].rearrange(pairs, t=2), root[k][:].rearrange(pairs, t=2), ALU.mult)
 
         w2_bf = keep.tile([P, N, PACK], BF16, name="w2_bf", align_bytes=64)
         w2_codes = keep.tile([P, N], U32, name="w2_codes", align_bytes=64)
@@ -189,13 +230,12 @@ def tile_picked_rsi4_none_p_kernel(tc, x_words, x_scales, w1, gn, w2, offs, t1, 
 
         def finish(ci, j0, width, z_planes):
             last_chunk = ci == len(CHUNKS) - 1
-            z_bf = keep.tile([P, width, PACK], BF16, name="z_bf%d" % ci, align_bytes=64)
-            dst = z_bf[:].rearrange("p (c i) t -> p c t i", i=4)
-            src = z_planes[:].rearrange("p t (c i) -> p c t i", i=4)
-            if last_chunk:
-                nc.vector.tensor_copy(dst, src)
-            else:
-                nc.scalar.copy(dst, src)
+            z_bf = z_words[ci]
+            if not last_chunk:
+                dst = z_bf[:].rearrange("p (c i) t -> p c t i", i=4)
+                src = z_planes[:].rearrange("p t (c i) -> p c t i", i=4)
+                for c0 in range(0, width // 4, 16):
+                    nc.scalar.copy(dst[:, c0 : c0 + 16], src[:, c0 : c0 + 16])
             z_codes = keep.tile([P, width], U32, name="z_codes%d" % ci, align_bytes=64)
             z_scales = keep.tile([P, width], U8, name="z_scales%d" % ci, align_bytes=64)
             nc.vector.quantize_mx(out=z_codes[:].bitcast(FP8X4), scales=z_scales[:], in_=z_bf[:].rearrange("p c t -> p (c t)"))
@@ -216,12 +256,35 @@ def tile_picked_rsi4_none_p_kernel(tc, x_words, x_scales, w1, gn, w2, offs, t1, 
                     nc.scalar.copy(flat, acc[:, 0 : per_bank * width])
                 nc.sync.dma_start(out_rows[:, m0 : m0 + per_bank, j0 : j0 + width], res[:])
 
-        z_all = [keep.tile([P, PACK, width], BF16, name="z_planes%d" % ci) for ci, width in enumerate(CHUNKS)]
+        z_all = [keep.tile([P, PACK, width], BF16, name="z_planes%d" % ci) for ci, width in enumerate(CHUNKS[:-1])]
+        z_words = [keep.tile([P, width, PACK], BF16, name="z_bf%d" % ci, align_bytes=64) for ci, width in enumerate(CHUNKS)]
         starts = [sum(CHUNKS[:ci]) for ci in range(len(CHUNKS))]
-        for step in STEPS:
-            if step[0] == "b":
-                block(starts[step[1]], CHUNKS[step[1]], step[2], z_all[step[1]])
-            elif step[0] == "w":
+        gather_a(0)
+        long_count = count - 2
+        for k in range(count):
+            if k >= 2 and k - 2 < long_count:
+                invert(k - 2)
+            front(k)
+            if k == 0:
+                project(2, "pr")
+            if k >= long_count:
+                close_early(k)
+            if k + 1 < count:
+                gather_a(k + 1)
+            if k >= 2:
+                scale(k - 2)
+            if k == 3:
                 quantise_w2()
-            else:
-                finish(step[1], starts[step[1]], CHUNKS[step[1]], z_all[step[1]])
+            if k == 5:
+                finish(0, starts[0], CHUNKS[0], z_all[0])
+            if k < long_count:
+                back(k)
+
+        short_ratio(count - 2)
+
+        short_ratio(count - 1)
+        finish(1, starts[1], CHUNKS[1], z_all[1])
+        short_scale(count - 2, z_words[2])
+        short_scale(count - 1, z_words[2])
+
+        finish(2, starts[2], CHUNKS[2], None)

@@ -18,11 +18,12 @@ ACT = mybir.ActivationFunctionType
 
 P = 128
 PACK = 4
-HALF = S // 2
+PER_COLUMN = 16
+BANK = 512
 BLOCK = 256
-CHUNKS = (256, 128, 128)
-W1_SPLIT = 40
-BLOCKS = ((0, (0,)), (0, (1,)), (0, (2,)), (0, (3,)), (1, (0, 1)), (1, (2, 3)), (2, (0, 1)), (2, (2, 3)))
+CHUNKS = S // BLOCK
+W1_VECTOR_SHARE = 40
+BANKS = {"rise": 2, "fall": 1, "sum": 3, "mx": 2}
 LAG = 2
 
 
@@ -34,9 +35,9 @@ def tile_picked_rsi4_none_p_kernel(tc, x_words, x_scales, w1, gn, w2, offs, t1, 
         psum = ctx.enter_context(tc.psum_pool(name="psum", bufs=1))
 
         def bank(tag):
-            return psum.tile([P, 512], F32, name=tag, tag=tag, bufs={"pr": 2, "rb": 1, "qu": 3, "acc": 2}[tag])
+            return psum.tile([P, BANK], F32, name=tag, tag=tag, bufs=BANKS[tag])
 
-        offs_sb = keep.tile([P, S // 16], U16, name="offs_sb")
+        offs_sb = keep.tile([P, S // PER_COLUMN], U16, name="offs_sb")
         nc.sync.dma_start(offs_sb[:], offs)
         xw = keep.tile([P, T], I32, name="xw", align_bytes=64)
         nc.sync.dma_start(xw[:], x_words[0].rearrange("p n t -> p (n t)").bitcast(I32))
@@ -50,18 +51,16 @@ def tile_picked_rsi4_none_p_kernel(tc, x_words, x_scales, w1, gn, w2, offs, t1, 
             raw = keep.tile([P, PACK, H // 2], F32, name="w1_raw%d" % h, tag="raw%d" % h)
             nc.sync.dma_start(raw[:], w1_rows[:, :, h * (H // 2) : (h + 1) * (H // 2)])
             w1_raw.append(raw)
-        lists = [keep.tile([P, S // 16], U16, name="list%d" % i) for i in range(4)]
-        for i, src in ((1, t2), (2, t3), (0, t1), (3, t4)):
-            nc.sync.dma_start(lists[i][:], src)
+        list_a, list_b, list_c, list_d = [keep.tile([P, S // PER_COLUMN], U16, name="list%d" % i) for i in range(4)]
+        for dst, src in ((list_b, t2), (list_c, t3), (list_a, t1), (list_d, t4)):
+            nc.sync.dma_start(dst[:], src)
         gain = keep.tile([P, PACK], F32, name="gain")
         nc.sync.dma_start(gain[:], gn.rearrange("(p t) o -> p (t o)", t=PACK))
 
-        ngain = keep.tile([P, PACK], F32, name="ngain")
-        nc.gpsimd.tensor_scalar(ngain[:], gain[:], -1.0, 0.0, ALU.mult, ALU.add)
-        warm = keep.tile([P, 1], F32, name="warm")
-        warm2 = keep.tile([P, 1], F32, name="warm2")
-        nc.vector.memset(warm[:], 1.0)
-        nc.scalar.activation(warm2[:], warm[:], ACT.Abs_reciprocal_sqrt)
+        sixteen = keep.tile([P, 1], F32, name="sixteen")
+        quarter = keep.tile([P, 1], F32, name="quarter")
+        nc.vector.memset(sixteen[:], 16.0)
+        nc.scalar.activation(quarter[:], sixteen[:], ACT.Abs_reciprocal_sqrt)
         ident = keep.tile([P, P], F32, name="ident", align_bytes=64)
         make_identity(nc, ident[:])
 
@@ -73,9 +72,10 @@ def tile_picked_rsi4_none_p_kernel(tc, x_words, x_scales, w1, gn, w2, offs, t1, 
         w1_bf = keep.tile([P, PACK * H], BF16, name="w1_bf", align_bytes=64)
         w1_view = w1_bf[:].rearrange("p (t m j) -> p m j t", t=PACK, j=PACK)
         w1_src = [raw[:].rearrange("p j (m t) -> p m j t", t=PACK) for raw in w1_raw]
-        nc.scalar.copy(w1_view[:, 0:64], w1_src[0])
-        nc.vector.tensor_copy(w1_view[:, 64 : 64 + W1_SPLIT], w1_src[1][:, 0:W1_SPLIT])
-        nc.scalar.copy(w1_view[:, 64 + W1_SPLIT : 128], w1_src[1][:, W1_SPLIT:64])
+        m_half = P // 2
+        nc.scalar.copy(w1_view[:, 0:m_half], w1_src[0])
+        nc.vector.tensor_copy(w1_view[:, m_half : m_half + W1_VECTOR_SHARE], w1_src[1][:, 0:W1_VECTOR_SHARE])
+        nc.scalar.copy(w1_view[:, m_half + W1_VECTOR_SHARE : P], w1_src[1][:, W1_VECTOR_SHARE:m_half])
         w1_codes = keep.tile([P, H], U32, name="w1_codes", align_bytes=64)
         w1_scales = keep.tile([P, H], U8, name="w1_scales", align_bytes=64)
         for f0, f1 in ((0, P), (P, 2 * P), (2 * P, 4 * P)):
@@ -85,206 +85,186 @@ def tile_picked_rsi4_none_p_kernel(tc, x_words, x_scales, w1, gn, w2, offs, t1, 
         nc.sync.dma_start(w2_raw[:], w2.rearrange("(p j) c -> p j c", j=PACK))
 
         y = [keep.tile([P, S], F32, name="y%d" % t) for t in range(PACK)]
-        yn = [keep.tile([P, S], F32, name="yn%d" % t) for t in range(PACK)]
-        halves = []
-        for h in range(2):
-            cols = slice(h * HALF, (h + 1) * HALF)
-            acc = bank("acc")
+        y_neg = [keep.tile([P, S], F32, name="y_neg%d" % t) for t in range(PACK)]
+
+        def product(acc, codes, scales, rows, rhs_codes, rhs_scales):
             nc.tensor.matmul_mx(
-                out=acc[:, 0:HALF], lhsT=w1_codes[:, 0:P].bitcast(FP8X4), lhsT_scale=w1_scales[:, 0:P],
-                rhs=xw_pick[:, cols].bitcast(FP8X4), rhs_scale=xs_pick[:, cols], start=True, stop=True,
+                out=acc, lhsT=codes[:, rows].bitcast(FP8X4), lhsT_scale=scales[:, rows],
+                rhs=rhs_codes.bitcast(FP8X4), rhs_scale=rhs_scales, start=True, stop=True,
             )
-            if h == 0:
-                nc.scalar.copy(y[0][:, cols], acc[:, 0:HALF])
-            else:
-                nc.vector.tensor_copy(y[0][:, cols], acc[:, 0:HALF])
-            halves.append((cols, acc))
-        for cols, acc in halves:
-            nc.scalar.activation(yn[0][:, cols], acc[:, 0:HALF], ACT.Copy, scale=-1.0)
+
         def project(t, tag):
             acc = bank(tag)
-            feats = slice(t * P, (t + 1) * P)
-            nc.tensor.matmul_mx(
-                out=acc[:], lhsT=w1_codes[:, feats].bitcast(FP8X4), lhsT_scale=w1_scales[:, feats],
-                rhs=xw_pick[:].bitcast(FP8X4), rhs_scale=xs_pick[:], start=True, stop=True,
-            )
+            product(acc[:], w1_codes, w1_scales, slice(t * P, (t + 1) * P), xw_pick[:], xs_pick[:])
             nc.scalar.copy(y[t][:], acc[:])
-            nc.scalar.activation(yn[t][:], acc[:], ACT.Copy, scale=-1.0)
+            nc.scalar.activation(y_neg[t][:], acc[:], ACT.Copy, scale=-1.0)
 
-        project(1, "qu")
+        halves = []
+        for h, copy in enumerate((nc.scalar.copy, nc.vector.tensor_copy)):
+            cols = slice(h * (S // 2), (h + 1) * (S // 2))
+            acc = bank("mx")[:, 0 : S // 2]
+            product(acc, w1_codes, w1_scales, slice(0, P), xw_pick[:, cols], xs_pick[:, cols])
+            copy(y[0][:, cols], acc)
+            halves.append((cols, acc))
+        for cols, acc in halves:
+            nc.scalar.activation(y_neg[0][:, cols], acc, ACT.Copy, scale=-1.0)
+        project(1, "sum")
+        project(3, "sum")
 
-        project(3, "qu")
+        count = CHUNKS * PACK
+        last_chunk = CHUNKS - 1
+        long_count = count - 2
+        low, high = slice(0, BLOCK), slice(BLOCK, 2 * BLOCK)
+        cells = [slice(c, c + P) for c in range(0, BLOCK, P)]
 
-        out_rows = out.rearrange("(mt p) j -> p mt j", p=P)
+        def fetch(planes, offsets, k):
+            first = k // PACK * (BLOCK // PER_COLUMN)
+            return planes[k % PACK][:].indirect(offsets[:, first : first + BLOCK // PER_COLUMN])
 
-        def add_transposed(dst, terms, cells):
+        def scratch(name, number):
+            return [keep.tile([P, BLOCK], F32, name="%s%d" % (name, k)) for k in range(number)]
+
+        def after(older, distance, name):
+            return scratch(name, distance) + older[: count - distance]
+
+        part3, den, root, rec = scratch("part3", count), scratch("den", count), scratch("root", long_count), scratch("rec", count)
+        b_a = after(den, LAG + 1, "b_a")
+        a_c = after(root, LAG + 1, "a_c")
+        neg_a = after(a_c, LAG + 1, "neg_a")
+        d_a = after(part3, LAG, "d_a")
+        up, parts = {}, {}
+
+        def add_transposed(dst, terms):
             for i, term in enumerate(terms):
-                for c in range(cells):
-                    cell = slice(c * P, (c + 1) * P)
+                for c, cell in enumerate(cells):
                     nc.tensor.matmul(
                         dst[:, cell], lhsT=term[:, cell], rhs=ident[:], is_transpose=True,
-                        start=(i == 0 and c == 0), stop=(i == len(terms) - 1 and c == cells - 1),
+                        start=(i == 0 and c == 0), stop=(i == len(terms) - 1 and c == len(cells) - 1),
                     )
 
-        def cut(k):
-            ci, planes = BLOCKS[k]
-            width = CHUNKS[ci]
-            lc = slice(starts[ci] // 16, (starts[ci] + width) // 16)
-            return [(t, slice(i * width, (i + 1) * width), lc) for i, t in enumerate(planes)], width * len(planes)
-
-        count = len(BLOCKS)
-        def scratch(name):
-            return [keep.tile([P, BLOCK], F32, name="%s%d" % (name, k)) for k in range(count)]
-        def after(older, lag, name):
-            return [older[k - lag] if k >= lag else keep.tile([P, BLOCK], F32, name="%s%d" % (name, k)) for k in range(count)]
-        up_r, den, root, rec = scratch("up_r"), scratch("den"), scratch("root"), scratch("rec")
-        ba = after(den, 3, "ba")
-        ac = after(root, 3, "ac")
-        da = after(up_r, 2, "da")
-        na = after(ac, 2, "na")
-
-        held = {}
-
         def gather_a(k):
-            for t, sp, lc in cut(k)[0]:
-                nc.vector.tensor_scalar(na[k][:, sp], y[t][:].indirect(lists[0][:, lc]), -1.0, 0.0, ALU.mult, ALU.add)
+            nc.vector.tensor_scalar(neg_a[k][:], fetch(y, list_a, k), -1.0, 0.0, ALU.mult, ALU.add)
 
-        def front(k):
-            spans, size = cut(k)
-            cells = size // P
-            for t, sp, lc in spans:
-                nc.vector.tensor_tensor(ba[k][:, sp], y[t][:].indirect(lists[1][:, lc]), na[k][:, sp], ALU.add)
-            for t, sp, lc in spans:
-                nc.vector.tensor_tensor(ac[k][:, sp], yn[t][:].indirect(lists[2][:, lc]), na[k][:, sp], ALU.subtract)
-            pr = bank("pr")
-            qu = bank("qu")
-            ups = work.tile([P, 2, BLOCK], F32, name="ups")
-            add_transposed(pr[:, 0:size], [ba[k]], cells)
-            nc.scalar.activation(ups[:, 0, 0:size], pr[:, 0:size], ACT.Relu, scale=-1.0)
-            add_transposed(qu[:, 0:size], [ba[k], ac[k]], cells)
-            nc.scalar.activation(ups[:, 1, 0:size], qu[:, 0:size], ACT.Relu)
-            held[k] = (pr, qu, ups)
+        def gather_d(k):
+            nc.vector.tensor_tensor(d_a[k][:], fetch(y, list_d, k), neg_a[k][:], ALU.add)
 
-        def back(k):
-            spans, size = cut(k)
-            cells = size // P
-            pr, qu, ups = held[k]
-            pr = bank("rb")
-            for t, sp, lc in spans:
-                nc.vector.tensor_tensor(da[k][:, sp], y[t][:].indirect(lists[3][:, lc]), na[k][:, sp], ALU.add)
-            add_transposed(pr[:, BLOCK : BLOCK + size], [ac[k], da[k]], cells)
-            nc.scalar.activation(up_r[k][:, 0:size], pr[:, BLOCK : BLOCK + size], ACT.Relu, scale=-1.0)
-            add_transposed(qu[:, BLOCK : BLOCK + size], [ups[:, 0, :], ups[:, 1, :], up_r[k]], cells)
+        def first_parts(k):
+            nc.vector.tensor_tensor(b_a[k][:], fetch(y, list_b, k), neg_a[k][:], ALU.add)
+            nc.vector.tensor_tensor(a_c[k][:], fetch(y_neg, list_c, k), neg_a[k][:], ALU.subtract)
+            rise = bank("rise")
+            total = bank("sum")
+            both = work.tile([P, 2, BLOCK], F32, name="both")
+            add_transposed(rise[:, low], [b_a[k]])
+            nc.scalar.activation(both[:, 0, :], rise[:, low], ACT.Relu, scale=-1.0)
+            add_transposed(total[:, low], [b_a[k], a_c[k]])
+            nc.scalar.activation(both[:, 1, :], total[:, low], ACT.Relu)
+            up[k], parts[k] = total[:, high], [both[:, 0, :], both[:, 1, :]]
+
+        def third_part(k):
+            fall = bank("fall")
+            gather_d(k)
+            add_transposed(fall[:, high], [a_c[k], d_a[k]])
+            nc.scalar.activation(part3[k][:], fall[:, high], ACT.Relu, scale=-1.0)
+            add_transposed(up[k], parts[k] + [part3[k]])
 
         def invert(k):
-            size = cut(k)[1]
-            up = held[k][1][:, BLOCK : BLOCK + size]
-            nc.vector.scalar_tensor_tensor(den[k][:, 0:size], up, 2.0, da[k][:, 0:size], ALU.mult, ALU.add)
-            nc.scalar.activation(root[k][:, 0:size], den[k][:, 0:size], ACT.Abs_reciprocal_sqrt, bias=0.25)
-            nc.scalar.activation(rec[k][:, 0:size], root[k][:, 0:size], ACT.Square)
+            nc.vector.scalar_tensor_tensor(den[k][:], up[k], 2.0, d_a[k][:], ALU.mult, ALU.add)
+            nc.scalar.activation(root[k][:], den[k][:], ACT.Abs_reciprocal_sqrt, bias=quarter[:])
+            nc.scalar.activation(rec[k][:], root[k][:], ACT.Square)
 
-        def scale(k):
-            spans, size = cut(k)
-            up = held[k][1][:, BLOCK : BLOCK + size]
-            for t, sp, lc in spans:
-                nc.vector.scalar_tensor_tensor(z_all[BLOCKS[k][0]][:, t, :], up[:, sp], gain[:, t : t + 1], rec[k][:, sp], ALU.mult, ALU.mult)
+        z_planes = [keep.tile([P, PACK, BLOCK], BF16, name="z_planes%d" % ci) for ci in range(CHUNKS)]
+        z_woven = [keep.tile([P, BLOCK, PACK], BF16, name="z_woven%d" % ci, align_bytes=64) for ci in range(CHUNKS)]
+        side_by_side = "p t j -> p j t"
 
-        def close_early(k):
-            size = cut(k)[1]
-            pr, qu, ups = held[k]
-            add_transposed(qu[:, BLOCK : BLOCK + size], [ups[:, 0, :], ups[:, 1, :]], size // P)
+        def write_z(k):
+            t = k % PACK
+            nc.vector.scalar_tensor_tensor(z_planes[k // PACK][:, t, :], up[k], gain[:, t : t + 1], rec[k][:], ALU.mult, ALU.mult)
 
-        def short_ratio(k):
-            spans, size = cut(k)
-            part = held[k][1][:, BLOCK : BLOCK + size]
-            dc, down = up_r[k], rec[k]
-            for t, sp, lc in spans:
-                nc.vector.tensor_tensor(da[k][:, sp], y[t][:].indirect(lists[3][:, lc]), na[k][:, sp], ALU.add)
-            for t, sp, lc in spans:
-                nc.vector.tensor_tensor(dc[:, sp], da[k][:, sp], ac[k][:, sp], ALU.add)
-            for t, sp, lc in spans:
-                nc.vector.scalar_tensor_tensor(down[:, sp], dc[:, sp], 0.0, part[:, sp], ALU.min, ALU.subtract)
-            for t, sp, lc in spans:
-                nc.vector.scalar_tensor_tensor(den[k][:, sp], down[:, sp], -2.0, da[k][:, sp], ALU.mult, ALU.add)
-            for t, sp, lc in spans:
-                nc.scalar.activation(root[k][:, sp], den[k][:, sp], ACT.Abs_reciprocal_sqrt, bias=0.25)
+        def weave_pair(k):
+            ci, pair = k // PACK, slice(k % PACK - 1, k % PACK + 1)
+            for cell in cells:
+                nc.scalar.copy(z_woven[ci][:, cell, pair], z_planes[ci][:, pair, cell].rearrange(side_by_side))
 
-        def short_scale(k, z_bf):
-            spans, size = cut(k)
-            down, once = rec[k], up_r[k]
-            for t, sp, lc in spans:
-                nc.vector.scalar_tensor_tensor(once[:, sp], down[:, sp], ngain[:, t : t + 1], root[k][:, sp], ALU.mult, ALU.mult)
-            t0 = spans[0][0]
-            pairs = "p (t j) -> p j t"
-            nc.vector.tensor_tensor(z_bf[:, :, t0 : t0 + 2], once[:].rearrange(pairs, t=2), root[k][:].rearrange(pairs, t=2), ALU.mult)
+        short_roots = keep.tile([P, 2, BLOCK], F32, name="short_roots")
+        short_once = keep.tile([P, 2, BLOCK], F32, name="short_once")
+
+        def short_root(k):
+            gather_d(k)
+            for cell in cells:
+                nc.vector.tensor_tensor(part3[k][:, cell], d_a[k][:, cell], a_c[k][:, cell], ALU.add)
+            for cell in cells:
+                nc.vector.scalar_tensor_tensor(rec[k][:, cell], part3[k][:, cell], 0.0, up[k][:, cell], ALU.min, ALU.subtract)
+            for cell in cells:
+                nc.vector.scalar_tensor_tensor(den[k][:, cell], rec[k][:, cell], -2.0, d_a[k][:, cell], ALU.mult, ALU.add)
+            for cell in cells:
+                nc.scalar.activation(short_roots[:, k - long_count, cell], den[k][:, cell], ACT.Abs_reciprocal_sqrt, bias=quarter[:])
+
+        def short_scale(k, cols):
+            t, i = k % PACK, k - long_count
+            nc.vector.scalar_tensor_tensor(short_once[:, i, cols], rec[k][:, cols], gain[:, t : t + 1], short_roots[:, i, cols], ALU.mult, ALU.mult)
+
+        def short_z(cols):
+            nc.vector.scalar_tensor_tensor(
+                z_woven[last_chunk][:, cols, PACK - 2 : PACK], short_once[:, :, cols].rearrange(side_by_side), -1.0,
+                short_roots[:, :, cols].rearrange(side_by_side), ALU.mult, ALU.mult,
+            )
 
         w2_bf = keep.tile([P, N, PACK], BF16, name="w2_bf", align_bytes=64)
         w2_codes = keep.tile([P, N], U32, name="w2_codes", align_bytes=64)
         w2_scales = keep.tile([P, N], U8, name="w2_scales", align_bytes=64)
 
         def quantise_w2():
-            for mt in range(N // P):
-                cols = slice(mt * P, (mt + 1) * P)
-                nc.scalar.copy(w2_bf[:, cols, :].rearrange("p (c i) j -> p c j i", i=4), w2_raw[:, :, cols].rearrange("p j (c i) -> p c j i", i=4))
+            for c0 in range(0, N, P):
+                nc.scalar.copy(
+                    w2_bf[:, c0 : c0 + P, :].rearrange("p (c i) j -> p c j i", i=4),
+                    w2_raw[:, :, c0 : c0 + P].rearrange("p j (c i) -> p c j i", i=4),
+                )
             nc.vector.quantize_mx(out=w2_codes[:].bitcast(FP8X4), scales=w2_scales[:], in_=w2_bf[:].rearrange("p c j -> p (c j)"))
 
-        def finish(ci, j0, width, z_planes):
-            last_chunk = ci == len(CHUNKS) - 1
-            z_bf = z_words[ci]
-            if not last_chunk:
-                dst = z_bf[:].rearrange("p (c i) t -> p c t i", i=4)
-                src = z_planes[:].rearrange("p t (c i) -> p c t i", i=4)
-                for c0 in range(0, width // 4, 16):
-                    nc.scalar.copy(dst[:, c0 : c0 + 16], src[:, c0 : c0 + 16])
-            z_codes = keep.tile([P, width], U32, name="z_codes%d" % ci, align_bytes=64)
-            z_scales = keep.tile([P, width], U8, name="z_scales%d" % ci, align_bytes=64)
-            nc.vector.quantize_mx(out=z_codes[:].bitcast(FP8X4), scales=z_scales[:], in_=z_bf[:].rearrange("p c t -> p (c t)"))
-            per_bank = 2 if last_chunk else 512 // width
-            for m0 in range(0, N // P, per_bank):
-                acc = bank("acc")
-                res = keep.tile([P, per_bank, width], F32, name="res%d_%d" % (ci, m0))
-                for i in range(per_bank):
-                    rows = slice((m0 + i) * P, (m0 + i + 1) * P)
-                    nc.tensor.matmul_mx(
-                        out=acc[:, i * width : (i + 1) * width], lhsT=w2_codes[:, rows].bitcast(FP8X4), lhsT_scale=w2_scales[:, rows],
-                        rhs=z_codes[:].bitcast(FP8X4), rhs_scale=z_scales[:], start=True, stop=True,
-                    )
-                flat = res[:].rearrange("p m j -> p (m j)")
-                if last_chunk and m0 > 0:
-                    nc.vector.tensor_copy(flat, acc[:, 0 : per_bank * width])
-                else:
-                    nc.scalar.copy(flat, acc[:, 0 : per_bank * width])
-                nc.sync.dma_start(out_rows[:, m0 : m0 + per_bank, j0 : j0 + width], res[:])
+        out_rows = out.rearrange("(mt p) j -> p mt j", p=P)
 
-        z_all = [keep.tile([P, PACK, width], BF16, name="z_planes%d" % ci) for ci, width in enumerate(CHUNKS[:-1])]
-        z_words = [keep.tile([P, width, PACK], BF16, name="z_bf%d" % ci, align_bytes=64) for ci, width in enumerate(CHUNKS)]
-        starts = [sum(CHUNKS[:ci]) for ci in range(len(CHUNKS))]
+        def finish(ci, cols, tag, copies):
+            width, j0 = cols.stop - cols.start, ci * BLOCK + cols.start
+            z_codes = keep.tile([P, width], U32, name="z_codes%d" % j0, align_bytes=64)
+            z_scales = keep.tile([P, width], U8, name="z_scales%d" % j0, align_bytes=64)
+            nc.vector.quantize_mx(out=z_codes[:].bitcast(FP8X4), scales=z_scales[:], in_=z_woven[ci][:, cols, :].rearrange("p c t -> p (c t)"))
+            for m0, copy in zip(range(0, N // P, 2), copies):
+                acc = bank(tag)
+                res = keep.tile([P, 2, width], F32, name="res%d_%d" % (j0, m0))
+                for i in range(2):
+                    rows = slice((m0 + i) * P, (m0 + i + 1) * P)
+                    product(acc[:, i * width : (i + 1) * width], w2_codes, w2_scales, rows, z_codes[:], z_scales[:])
+                copy(res[:].rearrange("p m j -> p (m j)"), acc[:, 0 : 2 * width])
+                nc.sync.dma_start(out_rows[:, m0 : m0 + 2, j0 : j0 + width], res[:])
+
         gather_a(0)
-        long_count = count - 2
         for k in range(count):
-            if k >= 2 and k - 2 < long_count:
-                invert(k - 2)
-            front(k)
+            done = k - LAG
+            if done >= 0:
+                invert(done)
+            first_parts(k)
             if k == 0:
-                project(2, "pr")
+                project(2, "rise")
             if k >= long_count:
-                close_early(k)
+                add_transposed(up[k], parts[k])
             if k + 1 < count:
                 gather_a(k + 1)
-            if k >= 2:
-                scale(k - 2)
-            if k == 3:
+            if done >= 0:
+                write_z(done)
+            if done in (1, PACK - 1):
+                weave_pair(done)
+            if k == PACK - 1:
                 quantise_w2()
-            if k == 5:
-                finish(0, starts[0], CHUNKS[0], z_all[0])
+            if done == PACK - 1:
+                finish(0, low, "mx", (nc.scalar.copy, nc.scalar.copy))
             if k < long_count:
-                back(k)
-
-        short_ratio(count - 2)
-
-        short_ratio(count - 1)
-        finish(1, starts[1], CHUNKS[1], z_all[1])
-        short_scale(count - 2, z_words[2])
-        short_scale(count - 1, z_words[2])
-
-        finish(2, starts[2], CHUNKS[2], None)
+                third_part(k)
+        for k in range(long_count, count):
+            short_root(k)
+        weave_pair(long_count - 1)
+        short_scale(count - 2, low)
+        for cell in cells:
+            short_scale(count - 1, cell)
+        for cell, tag in zip(cells, ("mx", "rise")):
+            short_z(cell)
+            finish(last_chunk, cell, tag, (nc.scalar.copy, nc.vector.tensor_copy))

@@ -23,7 +23,7 @@ BANK = 512
 BLOCK = 256
 CHUNKS = S // BLOCK
 W1_VECTOR_SHARE = 40
-BANKS = {"rise": 2, "fall": 1, "sum": 3, "mx": 2}
+BANKS = {"rise": 2, "fall": 1, "sum": 4, "mx": 1}
 LAG = 2
 
 
@@ -100,9 +100,9 @@ def tile_picked_rsi4_none_p_kernel(tc, x_words, x_scales, w1, gn, w2, offs, t1, 
             nc.scalar.activation(y_neg[t][:], acc[:], ACT.Copy, scale=-1.0)
 
         halves = []
-        for h, copy in enumerate((nc.scalar.copy, nc.vector.tensor_copy)):
+        for h, (tag, copy) in enumerate((("mx", nc.scalar.copy), ("fall", nc.vector.tensor_copy))):
             cols = slice(h * (S // 2), (h + 1) * (S // 2))
-            acc = bank("mx")[:, 0 : S // 2]
+            acc = bank(tag)[:, 0 : S // 2]
             product(acc, w1_codes, w1_scales, slice(0, P), xw_pick[:, cols], xs_pick[:, cols])
             copy(y[0][:, cols], acc)
             halves.append((cols, acc))
@@ -127,9 +127,11 @@ def tile_picked_rsi4_none_p_kernel(tc, x_words, x_scales, w1, gn, w2, offs, t1, 
         def after(older, distance, name):
             return scratch(name, distance) + older[: count - distance]
 
-        part3, den, root, rec = scratch("part3", count), scratch("den", count), scratch("root", long_count), scratch("rec", count)
-        b_a = after(den, LAG + 1, "b_a")
-        a_c = after(root, LAG + 1, "a_c")
+        first_res = [keep.tile([P, 2, BLOCK], F32, name="first_res%d" % i)[:] for i in range(2)]
+        part3, root, rec = scratch("part3", long_count), scratch("root", long_count), scratch("rec", long_count)
+        den = scratch("den", count - 1) + [first_res[1][:, 0, :]]
+        b_a = after(den, LAG + 1, "b_a")[:-1] + scratch("last_b_a", 1)
+        a_c = after(root, LAG + 1, "a_c")[:-1] + scratch("last_a_c", 1)
         neg_a = after(a_c, LAG + 1, "neg_a")
         d_a = after(part3, LAG, "d_a")
         up, parts = {}, {}
@@ -187,21 +189,24 @@ def tile_picked_rsi4_none_p_kernel(tc, x_words, x_scales, w1, gn, w2, offs, t1, 
 
         short_roots = keep.tile([P, 2, BLOCK], F32, name="short_roots")
         short_once = keep.tile([P, 2, BLOCK], F32, name="short_once")
+        d_c, neg_up = scratch("d_c", 2), scratch("neg_up", 2)
 
         def short_root(k):
+            i = k - long_count
             gather_d(k)
-            for cell in cells:
-                nc.vector.tensor_tensor(part3[k][:, cell], d_a[k][:, cell], a_c[k][:, cell], ALU.add)
-            for cell in cells:
-                nc.vector.scalar_tensor_tensor(rec[k][:, cell], part3[k][:, cell], 0.0, up[k][:, cell], ALU.min, ALU.subtract)
-            for cell in cells:
-                nc.vector.scalar_tensor_tensor(den[k][:, cell], rec[k][:, cell], -2.0, d_a[k][:, cell], ALU.mult, ALU.add)
-            for cell in cells:
-                nc.scalar.activation(short_roots[:, k - long_count, cell], den[k][:, cell], ACT.Abs_reciprocal_sqrt, bias=quarter[:])
+            steps = cells if k == count - 1 else [low]
+            for cell in steps:
+                nc.vector.tensor_tensor(d_c[i][:, cell], d_a[k][:, cell], a_c[k][:, cell], ALU.add)
+            for cell in steps:
+                nc.vector.scalar_tensor_tensor(neg_up[i][:, cell], d_c[i][:, cell], 0.0, up[k][:, cell], ALU.min, ALU.subtract)
+            for cell in steps:
+                nc.vector.scalar_tensor_tensor(den[k][:, cell], neg_up[i][:, cell], -2.0, d_a[k][:, cell], ALU.mult, ALU.add)
+            for cell in steps:
+                nc.scalar.activation(short_roots[:, i, cell], den[k][:, cell], ACT.Abs_reciprocal_sqrt, bias=quarter[:])
 
         def short_scale(k, cols):
             t, i = k % PACK, k - long_count
-            nc.vector.scalar_tensor_tensor(short_once[:, i, cols], rec[k][:, cols], gain[:, t : t + 1], short_roots[:, i, cols], ALU.mult, ALU.mult)
+            nc.vector.scalar_tensor_tensor(short_once[:, i, cols], neg_up[i][:, cols], gain[:, t : t + 1], short_roots[:, i, cols], ALU.mult, ALU.mult)
 
         def short_z(cols):
             nc.vector.scalar_tensor_tensor(
@@ -223,19 +228,22 @@ def tile_picked_rsi4_none_p_kernel(tc, x_words, x_scales, w1, gn, w2, offs, t1, 
 
         out_rows = out.rearrange("(mt p) j -> p mt j", p=P)
 
-        def finish(ci, cols, tag, copies):
+        def quantise_z(ci, cols):
             width, j0 = cols.stop - cols.start, ci * BLOCK + cols.start
             z_codes = keep.tile([P, width], U32, name="z_codes%d" % j0, align_bytes=64)
             z_scales = keep.tile([P, width], U8, name="z_scales%d" % j0, align_bytes=64)
             nc.vector.quantize_mx(out=z_codes[:].bitcast(FP8X4), scales=z_scales[:], in_=z_woven[ci][:, cols, :].rearrange("p c t -> p (c t)"))
-            for m0, copy in zip(range(0, N // P, 2), copies):
+            return z_codes, z_scales, width, j0
+
+        def finish(quantised, tags, copies, staging):
+            z_codes, z_scales, width, j0 = quantised
+            for m0, tag, copy, res in zip(range(0, N // P, 2), tags, copies, staging):
                 acc = bank(tag)
-                res = keep.tile([P, 2, width], F32, name="res%d_%d" % (j0, m0))
                 for i in range(2):
                     rows = slice((m0 + i) * P, (m0 + i + 1) * P)
                     product(acc[:, i * width : (i + 1) * width], w2_codes, w2_scales, rows, z_codes[:], z_scales[:])
-                copy(res[:].rearrange("p m j -> p (m j)"), acc[:, 0 : 2 * width])
-                nc.sync.dma_start(out_rows[:, m0 : m0 + 2, j0 : j0 + width], res[:])
+                copy(res.rearrange("p m j -> p (m j)"), acc[:, 0 : 2 * width])
+                nc.sync.dma_start(out_rows[:, m0 : m0 + 2, j0 : j0 + width], res)
 
         gather_a(0)
         for k in range(count):
@@ -256,15 +264,17 @@ def tile_picked_rsi4_none_p_kernel(tc, x_words, x_scales, w1, gn, w2, offs, t1, 
             if k == PACK - 1:
                 quantise_w2()
             if done == PACK - 1:
-                finish(0, low, "mx", (nc.scalar.copy, nc.scalar.copy))
+                first_chunk = quantise_z(0, low)
             if k < long_count:
                 third_part(k)
         for k in range(long_count, count):
             short_root(k)
+        finish(first_chunk, ("sum", "sum"), (nc.scalar.copy, nc.scalar.copy), first_res)
         weave_pair(long_count - 1)
         short_scale(count - 2, low)
         for cell in cells:
             short_scale(count - 1, cell)
-        for cell, tag in zip(cells, ("mx", "rise")):
+        for cell, tags in zip(cells, (("rise", "rise"), ("mx", "fall"))):
             short_z(cell)
-            finish(last_chunk, cell, tag, (nc.scalar.copy, nc.vector.tensor_copy))
+            last_res = [keep.tile([P, 2, P], F32, name="last_res%d_%d" % (cell.start, i))[:] for i in range(2)]
+            finish(quantise_z(last_chunk, cell), tags, (nc.scalar.copy, nc.vector.tensor_copy), last_res)

from contextlib import ExitStack

import concourse.mybir as mybir
from concourse.masks import make_identity

K, T, S, N, H = 512, 2048, 512, 512, 512
FLOPS = 2 * K * H * S + 2 * H * N * S

F32 = mybir.dt.float32
BF16 = mybir.dt.bfloat16
I32 = mybir.dt.int32
U32 = mybir.dt.uint32
U16 = mybir.dt.uint16
U8 = mybir.dt.uint8
FP8X4 = mybir.dt.float8_e4m3fn_x4
ALU = mybir.AluOpType
ACT = mybir.ActivationFunctionType

P = 128
PACK = 4
PER_COLUMN = 16
BANK = 512
BLOCK = 256
CHUNKS = S // BLOCK
W1_VECTOR_SHARE = 40
BANKS = {"rise": 2, "fall": 1, "sum": 4, "mx": 1}
LAG = 2


def tile_picked_rsi4_none_p_kernel(tc, x_words, x_scales, w1, gn, w2, offs, t1, t2, t3, t4, out):
    nc = tc.nc
    with ExitStack() as ctx:
        keep = ctx.enter_context(tc.tile_pool(name="keep", bufs=1))
        work = ctx.enter_context(tc.tile_pool(name="work", bufs=3))
        psum = ctx.enter_context(tc.psum_pool(name="psum", bufs=1))

        def bank(tag):
            return psum.tile([P, BANK], F32, name=tag, tag=tag, bufs=BANKS[tag])

        offs_sb = keep.tile([P, S // PER_COLUMN], U16, name="offs_sb")
        nc.sync.dma_start(offs_sb[:], offs)
        xw = keep.tile([P, T], I32, name="xw", align_bytes=64)
        nc.sync.dma_start(xw[:], x_words[0].rearrange("p n t -> p (n t)").bitcast(I32))
        xs = keep.tile([P, T], U8, name="xs", align_bytes=64)
        nc.vector.memset(xs[:].bitcast(I32), 0)
        for q in range(4):
            nc.sync.dma_start(xs[32 * q : 32 * q + 4, :].bitcast(I32), x_scales[0][4 * q : 4 * q + 4, :].bitcast(I32))
        w1_rows = w1.rearrange("(p j) c -> p j c", j=PACK)
        w1_raw = []
        for h in range(2):
            raw = keep.tile([P, PACK, H // 2], F32, name="w1_raw%d" % h, tag="raw%d" % h)
            nc.sync.dma_start(raw[:], w1_rows[:, :, h * (H // 2) : (h + 1) * (H // 2)])
            w1_raw.append(raw)
        list_a, list_b, list_c, list_d = [keep.tile([P, S // PER_COLUMN], U16, name="list%d" % i) for i in range(4)]
        for dst, src in ((list_b, t2), (list_c, t3), (list_a, t1), (list_d, t4)):
            nc.sync.dma_start(dst[:], src)
        gain = keep.tile([P, PACK], F32, name="gain")
        nc.sync.dma_start(gain[:], gn.rearrange("(p t) o -> p (t o)", t=PACK))

        sixteen = keep.tile([P, 1], F32, name="sixteen")
        quarter = keep.tile([P, 1], F32, name="quarter")
        nc.vector.memset(sixteen[:], 16.0)
        nc.scalar.activation(quarter[:], sixteen[:], ACT.Abs_reciprocal_sqrt)
        ident = keep.tile([P, P], F32, name="ident", align_bytes=64)
        make_identity(nc, ident[:])

        xw_pick = keep.tile([P, S], U32, name="xw_pick", align_bytes=64)
        nc.vector.tensor_copy(xw_pick[:], xw[:].bitcast(U32).indirect(offs_sb[:]))
        xs_pick = keep.tile([P, S], U8, name="xs_pick", align_bytes=64)
        nc.vector.tensor_copy(xs_pick[:], xs[:].indirect(offs_sb[:]))

        w1_bf = keep.tile([P, PACK * H], BF16, name="w1_bf", align_bytes=64)
        w1_view = w1_bf[:].rearrange("p (t m j) -> p m j t", t=PACK, j=PACK)
        w1_src = [raw[:].rearrange("p j (m t) -> p m j t", t=PACK) for raw in w1_raw]
        m_half = P // 2
        nc.scalar.copy(w1_view[:, 0:m_half], w1_src[0])
        nc.vector.tensor_copy(w1_view[:, m_half : m_half + W1_VECTOR_SHARE], w1_src[1][:, 0:W1_VECTOR_SHARE])
        nc.scalar.copy(w1_view[:, m_half + W1_VECTOR_SHARE : P], w1_src[1][:, W1_VECTOR_SHARE:m_half])
        w1_codes = keep.tile([P, H], U32, name="w1_codes", align_bytes=64)
        w1_scales = keep.tile([P, H], U8, name="w1_scales", align_bytes=64)
        for f0, f1 in ((0, P), (P, 2 * P), (2 * P, 4 * P)):
            nc.vector.quantize_mx(out=w1_codes[:, f0:f1].bitcast(FP8X4), scales=w1_scales[:, f0:f1], in_=w1_bf[:, PACK * f0 : PACK * f1])

        w2_raw = keep.tile([P, PACK, N], F32, name="w2_raw", tag="raw0")
        nc.sync.dma_start(w2_raw[:], w2.rearrange("(p j) c -> p j c", j=PACK))

        y = [keep.tile([P, S], F32, name="y%d" % t) for t in range(PACK)]
        y_neg = [keep.tile([P, S], F32, name="y_neg%d" % t) for t in range(PACK)]

        def product(acc, codes, scales, rows, rhs_codes, rhs_scales):
            nc.tensor.matmul_mx(
                out=acc, lhsT=codes[:, rows].bitcast(FP8X4), lhsT_scale=scales[:, rows],
                rhs=rhs_codes.bitcast(FP8X4), rhs_scale=rhs_scales, start=True, stop=True,
            )

        def project(t, tag):
            acc = bank(tag)
            product(acc[:], w1_codes, w1_scales, slice(t * P, (t + 1) * P), xw_pick[:], xs_pick[:])
            nc.scalar.copy(y[t][:], acc[:])
            nc.scalar.activation(y_neg[t][:], acc[:], ACT.Copy, scale=-1.0)

        halves = []
        for h, (tag, copy) in enumerate((("mx", nc.scalar.copy), ("fall", nc.vector.tensor_copy))):
            cols = slice(h * (S // 2), (h + 1) * (S // 2))
            acc = bank(tag)[:, 0 : S // 2]
            product(acc, w1_codes, w1_scales, slice(0, P), xw_pick[:, cols], xs_pick[:, cols])
            copy(y[0][:, cols], acc)
            halves.append((cols, acc))
        for cols, acc in halves:
            nc.scalar.activation(y_neg[0][:, cols], acc, ACT.Copy, scale=-1.0)
        project(1, "sum")
        project(3, "sum")

        count = CHUNKS * PACK
        last_chunk = CHUNKS - 1
        long_count = count - 2
        low, high = slice(0, BLOCK), slice(BLOCK, 2 * BLOCK)
        cells = [slice(c, c + P) for c in range(0, BLOCK, P)]

        def fetch(planes, offsets, k):
            first = k // PACK * (BLOCK // PER_COLUMN)
            return planes[k % PACK][:].indirect(offsets[:, first : first + BLOCK // PER_COLUMN])

        def scratch(name, number):
            return [keep.tile([P, BLOCK], F32, name="%s%d" % (name, k)) for k in range(number)]

        def after(older, distance, name):
            return scratch(name, distance) + older[: count - distance]

        first_res = [keep.tile([P, 2, BLOCK], F32, name="first_res%d" % i)[:] for i in range(2)]
        part3, root, rec = scratch("part3", long_count), scratch("root", long_count), scratch("rec", long_count)
        den = scratch("den", count - 1) + [first_res[1][:, 0, :]]
        b_a = after(den, LAG + 1, "b_a")[:-1] + scratch("last_b_a", 1)
        a_c = after(root, LAG + 1, "a_c")[:-1] + scratch("last_a_c", 1)
        neg_a = after(a_c, LAG + 1, "neg_a")
        d_a = after(part3, LAG, "d_a")
        up, parts = {}, {}

        def add_transposed(dst, terms):
            for i, term in enumerate(terms):
                for c, cell in enumerate(cells):
                    nc.tensor.matmul(
                        dst[:, cell], lhsT=term[:, cell], rhs=ident[:], is_transpose=True,
                        start=(i == 0 and c == 0), stop=(i == len(terms) - 1 and c == len(cells) - 1),
                    )

        def gather_a(k):
            nc.vector.tensor_scalar(neg_a[k][:], fetch(y, list_a, k), -1.0, 0.0, ALU.mult, ALU.add)

        def gather_d(k):
            nc.vector.tensor_tensor(d_a[k][:], fetch(y, list_d, k), neg_a[k][:], ALU.add)

        def first_parts(k):
            nc.vector.tensor_tensor(b_a[k][:], fetch(y, list_b, k), neg_a[k][:], ALU.add)
            nc.vector.tensor_tensor(a_c[k][:], fetch(y_neg, list_c, k), neg_a[k][:], ALU.subtract)
            rise = bank("rise")
            total = bank("sum")
            both = work.tile([P, 2, BLOCK], F32, name="both")
            add_transposed(rise[:, low], [b_a[k]])
            nc.scalar.activation(both[:, 0, :], rise[:, low], ACT.Relu, scale=-1.0)
            add_transposed(total[:, low], [b_a[k], a_c[k]])
            nc.scalar.activation(both[:, 1, :], total[:, low], ACT.Relu)
            up[k], parts[k] = total[:, high], [both[:, 0, :], both[:, 1, :]]

        def third_part(k):
            fall = bank("fall")
            gather_d(k)
            add_transposed(fall[:, high], [a_c[k], d_a[k]])
            nc.scalar.activation(part3[k][:], fall[:, high], ACT.Relu, scale=-1.0)
            add_transposed(up[k], parts[k] + [part3[k]])

        def invert(k):
            nc.vector.scalar_tensor_tensor(den[k][:], up[k], 2.0, d_a[k][:], ALU.mult, ALU.add)
            nc.scalar.activation(root[k][:], den[k][:], ACT.Abs_reciprocal_sqrt, bias=quarter[:])
            nc.scalar.activation(rec[k][:], root[k][:], ACT.Square)

        z_planes = [keep.tile([P, PACK, BLOCK], BF16, name="z_planes%d" % ci) for ci in range(CHUNKS)]
        z_woven = [keep.tile([P, BLOCK, PACK], BF16, name="z_woven%d" % ci, align_bytes=64) for ci in range(CHUNKS)]
        side_by_side = "p t j -> p j t"

        def write_z(k):
            t = k % PACK
            nc.vector.scalar_tensor_tensor(z_planes[k // PACK][:, t, :], up[k], gain[:, t : t + 1], rec[k][:], ALU.mult, ALU.mult)

        def weave_pair(k):
            ci, pair = k // PACK, slice(k % PACK - 1, k % PACK + 1)
            for cell in cells:
                nc.scalar.copy(z_woven[ci][:, cell, pair], z_planes[ci][:, pair, cell].rearrange(side_by_side))

        short_roots = keep.tile([P, 2, BLOCK], F32, name="short_roots")
        short_once = keep.tile([P, 2, BLOCK], F32, name="short_once")
        d_c, neg_up = scratch("d_c", 2), scratch("neg_up", 2)

        def short_root(k):
            i = k - long_count
            gather_d(k)
            steps = cells if k == count - 1 else [low]
            for cell in steps:
                nc.vector.tensor_tensor(d_c[i][:, cell], d_a[k][:, cell], a_c[k][:, cell], ALU.add)
            for cell in steps:
                nc.vector.scalar_tensor_tensor(neg_up[i][:, cell], d_c[i][:, cell], 0.0, up[k][:, cell], ALU.min, ALU.subtract)
            for cell in steps:
                nc.vector.scalar_tensor_tensor(den[k][:, cell], neg_up[i][:, cell], -2.0, d_a[k][:, cell], ALU.mult, ALU.add)
            for cell in steps:
                nc.scalar.activation(short_roots[:, i, cell], den[k][:, cell], ACT.Abs_reciprocal_sqrt, bias=quarter[:])

        def short_scale(k, cols):
            t, i = k % PACK, k - long_count
            nc.vector.scalar_tensor_tensor(short_once[:, i, cols], neg_up[i][:, cols], gain[:, t : t + 1], short_roots[:, i, cols], ALU.mult, ALU.mult)

        def short_z(cols):
            nc.vector.scalar_tensor_tensor(
                z_woven[last_chunk][:, cols, PACK - 2 : PACK], short_once[:, :, cols].rearrange(side_by_side), -1.0,
                short_roots[:, :, cols].rearrange(side_by_side), ALU.mult, ALU.mult,
            )

        w2_bf = keep.tile([P, N, PACK], BF16, name="w2_bf", align_bytes=64)
        w2_codes = keep.tile([P, N], U32, name="w2_codes", align_bytes=64)
        w2_scales = keep.tile([P, N], U8, name="w2_scales", align_bytes=64)

        def quantise_w2():
            for c0 in range(0, N, P):
                nc.scalar.copy(
                    w2_bf[:, c0 : c0 + P, :].rearrange("p (c i) j -> p c j i", i=4),
                    w2_raw[:, :, c0 : c0 + P].rearrange("p j (c i) -> p c j i", i=4),
                )
            nc.vector.quantize_mx(out=w2_codes[:].bitcast(FP8X4), scales=w2_scales[:], in_=w2_bf[:].rearrange("p c j -> p (c j)"))

        out_rows = out.rearrange("(mt p) j -> p mt j", p=P)

        def quantise_z(ci, cols):
            width, j0 = cols.stop - cols.start, ci * BLOCK + cols.start
            z_codes = keep.tile([P, width], U32, name="z_codes%d" % j0, align_bytes=64)
            z_scales = keep.tile([P, width], U8, name="z_scales%d" % j0, align_bytes=64)
            nc.vector.quantize_mx(out=z_codes[:].bitcast(FP8X4), scales=z_scales[:], in_=z_woven[ci][:, cols, :].rearrange("p c t -> p (c t)"))
            return z_codes, z_scales, width, j0

        def finish(quantised, tags, copies, staging):
            z_codes, z_scales, width, j0 = quantised
            for m0, tag, copy, res in zip(range(0, N // P, 2), tags, copies, staging):
                acc = bank(tag)
                for i in range(2):
                    rows = slice((m0 + i) * P, (m0 + i + 1) * P)
                    product(acc[:, i * width : (i + 1) * width], w2_codes, w2_scales, rows, z_codes[:], z_scales[:])
                copy(res.rearrange("p m j -> p (m j)"), acc[:, 0 : 2 * width])
                nc.sync.dma_start(out_rows[:, m0 : m0 + 2, j0 : j0 + width], res)

        gather_a(0)
        for k in range(count):
            done = k - LAG
            if done >= 0:
                invert(done)
            first_parts(k)
            if k == 0:
                project(2, "rise")
            if k >= long_count:
                add_transposed(up[k], parts[k])
            if k + 1 < count:
                gather_a(k + 1)
            if done >= 0:
                write_z(done)
            if done in (1, PACK - 1):
                weave_pair(done)
            if k == PACK - 1:
                quantise_w2()
            if done == PACK - 1:
                first_chunk = quantise_z(0, low)
            if k < long_count:
                third_part(k)
        for k in range(long_count, count):
            short_root(k)
        finish(first_chunk, ("sum", "sum"), (nc.scalar.copy, nc.scalar.copy), first_res)
        weave_pair(long_count - 1)
        short_scale(count - 2, low)
        for cell in cells:
            short_scale(count - 1, cell)
        for cell, tags in zip(cells, (("rise", "rise"), ("mx", "fall"))):
            short_z(cell)
            last_res = [keep.tile([P, 2, P], F32, name="last_res%d_%d" % (cell.start, i))[:] for i in range(2)]
            finish(quantise_z(last_chunk, cell), tags, (nc.scalar.copy, nc.vector.tensor_copy), last_res)
